import numpy as np
import ml_dtypes


def mxq(x, axis, fmt="e4m3"):
    dtype, down = {"e4m3": (ml_dtypes.float8_e4m3fn, 7), "e5m2": (ml_dtypes.float8_e5m2, 14)}[fmt]
    v = np.moveaxis(np.asarray(x, np.float32).astype(ml_dtypes.bfloat16).astype(np.float64), axis, -1)
    blocks = v.reshape(v.shape[:-1] + (-1, 32))
    amax = np.abs(blocks).max(-1, keepdims=True)
    byte = np.maximum(np.where(amax > 0, np.frexp(amax)[1] - 1 + 127, 0) - down, 1)
    scale = np.exp2(byte - 127.0)
    codes = (blocks / scale).astype(np.float32).astype(dtype).astype(np.float64)
    return np.moveaxis((codes * scale).reshape(v.shape), -1, axis)


WIDE = False


def mx_kscale(k):
    if not WIDE:
        return np.ones(k)
    levels = np.array([10, -10, 5, -5, 0])
    if k % 512:
        return np.exp2(np.random.permutation(np.resize(levels, k // 32))).repeat(32)
    a = np.empty((k // 512, 16))
    for p in range(k // 512):
        a[p, :8] = np.random.permutation(np.resize(levels, 8))
        for g in range(8):
            far = levels[np.abs(levels - a[p, g]) >= 10]
            a[p, g + 8] = far[np.random.randint(len(far))]
    return np.exp2(a.ravel()).repeat(32)


BF16 = ml_dtypes.bfloat16


def bf(x):
    return np.asarray(x, np.float32).astype(BF16)


def f64(x):
    return np.asarray(x).astype(np.float64)


E2M1 = np.array([0.0, 0.5, 1.0, 1.5, 2.0, 3.0, 4.0, 6.0, -0.0, -0.5, -1.0, -1.5, -2.0, -3.0, -4.0, -6.0])


def pack_weight(w, fmt):
    k, n = w.shape
    w = f64(bf(w)).reshape(k // 32, 32, n)
    amax = np.abs(w).max(1)
    if fmt == "e4m3":
        byte = np.frexp(amax)[1] - 1 + 127 - 7
    else:
        mant, ex = np.frexp(amax / 6.0)
        byte = np.where(mant > 0.5, ex, ex - 1) + 127
    byte = np.clip(np.where(amax > 0, byte, 1), 1, 254)
    scaled = (w * np.exp2(127.0 - byte)[:, None, :]).reshape(k, n).astype(np.float32)
    by_word = np.ascontiguousarray(scaled.reshape(k // 512, 128, 4, n).transpose(0, 1, 3, 2))
    if fmt == "e4m3":
        words = by_word.astype(ml_dtypes.float8_e4m3fn).view(np.uint8)
    else:
        c = by_word.astype(ml_dtypes.float4_e2m1fn).view(np.uint8) & 0xF
        words = c[..., 0::2] | (c[..., 1::2] << 4)
    return np.ascontiguousarray(words), np.ascontiguousarray(byte.astype(np.uint8).reshape(k // 512, 16, n))


def unpack_weight(words, scales, fmt):
    g, p, n, _ = words.shape
    if fmt == "e4m3":
        vals = np.ascontiguousarray(words).view(ml_dtypes.float8_e4m3fn).astype(np.float64)
    else:
        nib = np.empty((g, p, n, 4), np.uint8)
        nib[..., 0::2] = words & 0xF
        nib[..., 1::2] = words >> 4
        vals = E2M1[nib]
    vals = vals * np.repeat(np.exp2(scales.astype(np.float64) - 127.0), 8, axis=1)[..., None]
    return vals.transpose(0, 1, 3, 2).reshape(g * 512, n)
def pack4(w):
    words, scales = pack_weight(w, "e2m1")
    return words.reshape(words.shape[0], 128, -1), scales


def unpack4(words, scales):
    return unpack_weight(words.reshape(words.shape[0], 128, -1, 2), scales, "e2m1")


E4M3FN = np.array([(-1.0 if i & 128 else 1.0) * ((1.0 + (i & 7) / 8.0) * 2.0 ** (((i >> 3) & 15) - 7) if i & 120 else (i & 7) * 2.0 ** -9) for i in range(256)])


def e4m3fn_bytes(y):
    return np.clip(np.asarray(y, np.float64), -448.0, 448.0).astype(np.float32).astype(ml_dtypes.float8_e4m3fn).view(np.uint8)


def e4m3fn_values(b):
    return E4M3FN[b]


M, N, B = 1024, 1536, 128


def setup_inputs():
    s, t = mx_kscale(N), mx_kscale(M)
    grad = np.random.standard_normal((M, N)) * s * t[:, None]
    right = np.random.standard_normal((N, N)) / np.sqrt(N) / s[:, None]
    grad_scale = (np.abs(grad).reshape(M, N // B, B).max(axis=2) / 448).astype(np.float32)
    right_scale = (np.abs(right).reshape(N // B, B, N // B, B).max(axis=(1, 3)) / 448).astype(np.float32)
    grad_bytes = e4m3fn_bytes(grad / np.repeat(f64(grad_scale), B, axis=1))
    right_bytes = e4m3fn_bytes(right / np.repeat(np.repeat(f64(right_scale), B, axis=0), B, axis=1))
    lt_words, lt_scales = pack4(np.random.standard_normal((M, M)) / np.sqrt(M) / t[:, None])
    return {"grad_bytes": grad_bytes, "grad_scale": grad_scale,
            "right_bytes": right_bytes, "right_scale": right_scale,
            "step": bf(np.exp(0.4 * np.random.standard_normal(N))),
            "lt_words": lt_words, "lt_scales": lt_scales,
            "w": bf(np.random.standard_normal((M, N)))}


def reference(grad_bytes, grad_scale, right_bytes, right_scale, step, lt_words, lt_scales, w):
    grad = e4m3fn_values(grad_bytes) * np.repeat(f64(grad_scale), B, axis=1)
    right = e4m3fn_values(right_bytes) * np.repeat(np.repeat(f64(right_scale), B, axis=0), B, axis=1)
    h = (mxq(grad, 1, "e4m3") @ mxq(right, 0, "e4m3")) * f64(step)
    lt = unpack4(lt_words, lt_scales)
    u = lt.T @ mxq(h, 0, "e4m3")
    return f64(w) - u

from contextlib import ExitStack

import concourse.mybir as mybir
from concourse.masks import make_identity

M, N, B = 1024, 1536, 128
FLOPS = 2 * M * N * N + 2 * M * M * N

F32 = mybir.dt.float32
BF16 = mybir.dt.bfloat16
U32 = mybir.dt.uint32
I32 = mybir.dt.int32
U8 = mybir.dt.uint8
E4M3 = mybir.dt.float8_e4m3fn
E4M3X4 = mybir.dt.float8_e4m3fn_x4
E2M1X4 = mybir.dt.float4_e2m1fn_x4
MULT = mybir.AluOpType.mult
SUB = mybir.AluOpType.subtract
COPY = mybir.ActivationFunctionType.Copy

P = 128
G = M // 512
Q = N // 512
NB = N // B
VEC_SHARE = (4, 5, 8, 4, 2, 3, 3, 3, 4, 2, 4, 3)
GE_VEC = (2, 5, 9, 11)
OP_WIDE = (0, 1, 2, 4, 5, 6, 7, 8, 10, 11)
OP_NARROW = (0, 3)
CHUNKS = ((0, 1), (1, 1), (2, 1), (3, 1), (4, 1), (5, 1), (6, 1), (7, 1), (8, 1), (9, 1), (10, 1), (11, 1))
PATH = ("vvv", "vvv", "avv", "vva", "vav", "avv", "vva", "vav", "vvv", "vvv", "avv", "ava")
HEAD = {4: 3, 9: 3, 11: 2, 12: 1}
STEADY = {1: 1, 2: 4, 3: 1, 4: 2, 5: 4, 6: 5, 7: 2, 8: 4}
EARLY_S1 = 8


def tile_two_sided_preconditioned_step_d4_kernel(
        tc, grad_bytes, grad_scale, right_bytes, right_scale, step, lt_words, lt_scales, w, out):
    nc = tc.nc
    with ExitStack() as ctx:
        keep = ctx.enter_context(tc.tile_pool(name="keep", bufs=1))
        rot = ctx.enter_context(tc.tile_pool(name="rot", bufs=4))
        ps_h = ctx.enter_context(tc.psum_pool(name="ps_h", bufs=3))
        ps_o = ctx.enter_context(tc.psum_pool(name="ps_o", bufs=5))

        gb = grad_bytes.rearrange("(g p t) k -> g p t k", p=P, t=4)
        rb = right_bytes.rearrange("(q p t) n -> q p t n", p=P, t=4)
        ov = out.rearrange("(r p) n -> p r n", p=P)
        wv = w.rearrange("(r p) n -> p r n", p=P)

        gs = keep.tile([P, G, 4 * NB], F32, name="gs")
        nc.scalar.dma_start(out=gs[:], in_=grad_scale.rearrange("(g p t) c -> p g (t c)", p=P, t=4))

        ident = keep.tile([P, P], F32, name="ident")
        make_identity(nc, ident[:])
        lts = keep.tile([P, G, M], U8, name="lts", align_bytes=64)
        nc.gpsimd.memset(lts[:].rearrange("p g n -> p (g n)").bitcast(I32), 0)

        graw = [[keep.tile([P, 2, N], U8, name="graw%d%d" % (g, tp)) for tp in range(2)] for g in range(G)]
        rraw = [[keep.tile([P, 4, 512], U8, name="rraw%d%d" % (j, q)) for q in range(Q)] for j in range(3)]

        def load_grad(g, tp):
            nc.sync.dma_start(out=graw[g][tp][:], in_=gb[g][:, 2 * tp : 2 * tp + 2, :])

        def load_right(j, q):
            nc.sync.dma_start(out=rraw[j][q][:], in_=rb[q][:, :, 512 * j : 512 * j + 512])

        for q in range(Q):
            nc.sync.dma_start(out=graw[0][0][:, :, 512 * q : 512 * q + 512], in_=gb[0][:, 0:2, 512 * q : 512 * q + 512])
        load_grad(0, 1)
        rs_all = keep.tile([P, NB * NB], F32, name="rs_all")
        nc.sync.dma_start(out=rs_all[:], in_=right_scale.rearrange("a c -> (a c)").partition_broadcast(P))
        for q in range(Q):
            load_right(0, q)
        load_grad(1, 0)
        load_grad(1, 1)
        stepb = keep.tile([P, N], BF16, name="stepb")
        nc.sync.dma_start(out=stepb[:], in_=step.partition_broadcast(P))
        for q in range(Q):
            load_right(1, q)
        ltw = keep.tile([P, G, 2 * M], U8, name="ltw", align_bytes=64)
        for s in range(4):
            nc.sync.dma_start(out=lts[32 * s : 32 * s + 4, :, :].bitcast(I32),
                              in_=lt_scales.rearrange("g (s r) n -> s r g n", s=4)[s].bitcast(I32))
        nc.sync.dma_start(out=ltw[:], in_=lt_words.rearrange("g p n -> p g n"))
        for q in range(Q):
            load_right(2, q)
        w_sb = keep.tile([P, 8, N], BF16, name="w_sb")
        for r in range(0, 8, 2):
            nc.sync.dma_start(out=w_sb[:, r : r + 2, :], in_=wv[:, r : r + 2, :])

        rs = keep.tile([P, Q, NB], F32, name="rs")
        rs_v = rs_all[:].rearrange("p (q s c) -> p s q c", s=4, c=NB)
        for s in range(4):
            sl = slice(32 * s, 32 * s + 32)
            nc.gpsimd.tensor_copy(out=rs[sl, :, :], in_=rs_v[sl, s, :, :])

        gw = [[keep.tile([P, N], BF16, name="gw%d%d" % (g, t)) for t in range(4)] for g in range(G)]
        gc = {}
        gsc = {}
        units = [(g, tp, q) for g in range(G) for tp in range(2) for q in range(Q)]
        turned = {}

        def widen(u):
            g, tp, q = units[u]
            n = 0
            for tl in range(2):
                t = 2 * tp + tl
                for c in range(4 * q, 4 * q + 4):
                    src = graw[g][tp][:, tl, c * B : c * B + B].bitcast(E4M3)
                    dst = gw[g][t][:, c * B : c * B + B]
                    col = gs[:, g, t * NB + c : t * NB + c + 1]
                    if n % 8 in (0, 2, 4, 6, 7, 1, 3, 5)[:VEC_SHARE[u]]:
                        nc.vector.tensor_scalar(out=dst, in0=src, scalar1=col, scalar2=None, op0=MULT)
                    else:
                        nc.scalar.activation(out=dst, in_=src, func=COPY, scale=col)
                    n += 1

        def turn(u):
            g, tp, q = units[u]
            xt = ps_o.tile([P, 2, 2, P], F32, name="po")
            for tl in range(2):
                words = gw[g][2 * tp + tl][:].bitcast(F32)
                for e in range(2):
                    nc.tensor.transpose(xt[:, tl, e, :], words[:, 256 * q + e : 256 * (q + 1) : 2], ident[:])
            gx = rot.tile([P, 1024], BF16, name="gx", align_bytes=64)
            dst = gx[:].bitcast(F32).rearrange("p (t m e) -> p t m e", t=2, e=2)
            src = xt[:].rearrange("p t e m -> p t m e")
            if u in GE_VEC:
                nc.vector.tensor_copy(out=dst, in_=src)
            else:
                nc.scalar.copy(out=dst, in_=src)
            turned[u] = gx

        def quant_grad(u):
            key = units[u]
            c = keep.tile([P, 256], U32, name="gc%d" % u, align_bytes=64)
            s = keep.tile([P, 256], U8, name="gsc%d" % u, align_bytes=64)
            nc.vector.quantize_mx(out=c[:].bitcast(E4M3X4), scales=s[:], in_=turned[u][:])
            gc[key] = c
            gsc[key] = s

        rc = {}
        rsc = {}
        rjobs = [(k, q) for k in range(len(CHUNKS)) for q in range(Q)]
        rwide = {}

        def prep_right(k, q):
            i0, wd = CHUNKS[k]
            src = rraw[i0 // 4][q]
            off = B * (i0 % 4)
            wide = rot.tile([P, wd * 512], BF16, name="rw%d" % (wd * 10 + q), align_bytes=64, bufs=2)
            if PATH[k][q] == "a":
                for b in range(wd):
                    pl = rot.tile([P, 4, B], BF16, name="rp")
                    for t in range(4):
                        nc.scalar.activation(out=pl[:, t, :], in_=src[:, t, off + B * b : off + B * b + B].bitcast(E4M3),
                                             func=COPY, scale=rs[:, q, i0 + b : i0 + b + 1])
                    nc.scalar.copy(out=wide[:, 512 * b : 512 * b + 512].rearrange("p (n t) -> p n t", t=4), in_=pl[:].rearrange("p t n -> p n t"))
            else:
                eng = nc.vector if PATH[k][q] == "v" else nc.gpsimd
                il = rot.tile([P, wd * 512], U8, name="il%d" % (wd * 10 + q), align_bytes=64, bufs=2)
                eng.tensor_copy(out=il[:].rearrange("p (n t) -> p n t", t=4),
                                in_=src[:, :, off : off + B * wd].rearrange("p t n -> p n t"))
                for b in range(wd):
                    nc.scalar.activation(out=wide[:, 512 * b : 512 * b + 512], in_=il[:, 512 * b : 512 * b + 512].bitcast(E4M3),
                                         func=COPY, scale=rs[:, q, i0 + b : i0 + b + 1])
            rwide[k, q] = wide

        def quant_right(k, q):
            i0, wd = CHUNKS[k]
            c = keep.tile([P, B * wd], U32, name="rc%d_%d" % (k, q), align_bytes=64)
            s = keep.tile([P, B * wd], U8, name="rsc%d_%d" % (k, q), align_bytes=64)
            nc.vector.quantize_mx(out=c[:].bitcast(E4M3X4), scales=s[:], in_=rwide[k, q][:])
            for b in range(wd):
                rc[i0 + b, q] = c[:, B * b : B * b + B]
                rsc[i0 + b, q] = s[:, B * b : B * b + B]

        rpos = [0, 0]

        def right_step(n, lag):
            for x in range(n):
                if rpos[0] < len(rjobs):
                    prep_right(*rjobs[rpos[0]])
                    rpos[0] += 1
                while rpos[1] < rpos[0] - lag or (rpos[0] == len(rjobs) and lag == 0 and rpos[1] < len(rjobs)):
                    quant_right(*rjobs[rpos[1]])
                    rpos[1] += 1

        def right_ready(i):
            while (i, Q - 1) not in rc:
                if rpos[1] >= rpos[0]:
                    prep_right(*rjobs[rpos[0]])
                    rpos[0] += 1
                quant_right(*rjobs[rpos[1]])
                rpos[1] += 1

        h_ps = {}
        hb = {}
        hc = {}
        hs = {}
        for g in range(G):
            for j in range(3):
                hc[g, j] = keep.tile([P, 512], U32, name="hc%d%d" % (g, j), align_bytes=64)
                hs[g, j] = keep.tile([P, 512], U8, name="hs%d%d" % (g, j), align_bytes=64)

        def first(g, i):
            ps = ps_h.tile([P, 4, B], F32, name="ps")
            for t in range(4):
                m = slice(P * (t % 2), P * (t % 2) + P)
                for q in range(Q):
                    key = (g, t // 2, q)
                    nc.tensor.matmul_mx(
                        out=ps[:, t, :],
                        lhsT=gc[key][:, m].bitcast(E4M3X4), lhsT_scale=gsc[key][:, m],
                        rhs=rc[i, q].bitcast(E4M3X4), rhs_scale=rsc[i, q],
                        start=(q == 0), stop=(q == Q - 1))
            h_ps[g, i] = ps

        def make_h(g, i):
            t = rot.tile([P, 512], BF16, name="hb", align_bytes=64)
            nc.vector.tensor_tensor(
                out=t[:].rearrange("p (n t) -> p n t", t=4),
                in0=h_ps[g, i][:].rearrange("p t n -> p n t"),
                in1=stepb[:, B * i : B * i + B].unsqueeze(2).to_broadcast([P, B, 4]), op=MULT)
            hb[g, i] = t

        def quant_h(g, i):
            n = slice(B * (i % 4), B * (i % 4) + B)
            nc.vector.quantize_mx(out=hc[g, i // 4][:, n].bitcast(E4M3X4), scales=hs[g, i // 4][:, n], in_=hb[g, i][:])

        o_ps = {}

        def second(r, j):
            ps = ps_o.tile([P, 512], F32, name="po")
            for g in range(G):
                nc.tensor.matmul_mx(
                    out=ps[:],
                    lhsT=ltw[:, g, 256 * r : 256 * r + 256].bitcast(E2M1X4), lhsT_scale=lts[:, g, P * r : P * r + P],
                    rhs=hc[g, j][:].bitcast(E4M3X4), rhs_scale=hs[g, j][:], start=(g == 0), stop=(g == G - 1))
            o_ps[r, j] = ps

        def finish(r, j):
            o = rot.tile([P, 512], F32, name="ob")
            cols = slice(512 * j, 512 * j + 512)
            if (r + 8 * j) in OP_WIDE:
                u = rot.tile([P, 512], F32, name="ou")
                nc.scalar.copy(out=u[:], in_=o_ps[r, j][:])
                nc.gpsimd.tensor_tensor(out=o[:], in0=w_sb[:, r, cols], in1=u[:], op=SUB)
            else:
                nc.vector.tensor_tensor(out=o[:], in0=w_sb[:, r, cols], in1=o_ps[r, j][:], op=SUB)
            nc.sync.dma_start(out=ov[:, r, cols], in_=o[:])

        def second_narrow(half, i):
            ps = ps_o.tile([P, 4, B], F32, name="po")
            n = slice(B * (i % 4), B * (i % 4) + B)
            for rr in range(4):
                r = 4 * half + rr
                for g in range(G):
                    nc.tensor.matmul_mx(
                        out=ps[:, rr, :],
                        lhsT=ltw[:, g, 256 * r : 256 * r + 256].bitcast(E2M1X4), lhsT_scale=lts[:, g, P * r : P * r + P],
                        rhs=hc[g, i // 4][:, n].bitcast(E4M3X4), rhs_scale=hs[g, i // 4][:, n],
                        start=(g == 0), stop=(g == G - 1))
            o_ps[half, "n", i] = ps

        def finish_narrow(half, i):
            o = rot.tile([P, 4, B], F32, name="on")
            cols = slice(B * i, B * i + B)
            rows = slice(4 * half, 4 * half + 4)
            if (half + 2 * (i - 8)) in OP_NARROW:
                u = rot.tile([P, 4, B], F32, name="un")
                nc.scalar.copy(out=u[:], in_=o_ps[half, "n", i][:])
                nc.gpsimd.tensor_tensor(out=o[:], in0=w_sb[:, rows, cols], in1=u[:], op=SUB)
            else:
                nc.vector.tensor_tensor(out=o[:], in0=w_sb[:, rows, cols], in1=o_ps[half, "n", i][:], op=SUB)
            nc.sync.dma_start(out=ov[:, rows, cols], in_=o[:])

        nu = len(units)
        for s in range(nu + 2):
            if s < nu:
                widen(s)
            if 1 <= s < nu + 1:
                turn(s - 1)
            if s >= 2:
                quant_grad(s - 2)
            if s in HEAD:
                right_step(HEAD[s], 1)
            if s == EARLY_S1:
                right_ready(0)
                first(0, 0)
            if s == EARLY_S1 + 1:
                make_h(0, 0)

        for i in range(NB + 2):
            if i < NB:
                right_ready(i)
                if i > 0:
                    first(0, i)
                first(1, i)
            if 1 <= i <= NB:
                quant_h(0, i - 1)
                quant_h(1, i - 1)
            pend = []
            lo = 2 * (i - 4)
            if 0 <= lo < 16:
                pend = [(x % 8, x // 8) for x in range(lo, lo + 2)]
            for r, j in pend:
                second(r, j)
            if 9 <= i <= NB:
                second_narrow(0, i - 1)
                second_narrow(1, i - 1)
            right_step(STEADY.get(i, 0), 1)
            if i < NB:
                if i > 0:
                    make_h(0, i)
                make_h(1, i)
            for r, j in pend:
                finish(r, j)
            if 9 <= i <= NB:
                finish_narrow(0, i - 1)
                finish_narrow(1, i - 1)
